import numpy as np
import ml_dtypes


def mxq(x, axis, fmt="e4m3"):
    dtype, down = {"e4m3": (ml_dtypes.float8_e4m3fn, 7), "e5m2": (ml_dtypes.float8_e5m2, 14)}[fmt]
    v = np.moveaxis(np.asarray(x, np.float32).astype(ml_dtypes.bfloat16).astype(np.float64), axis, -1)
    blocks = v.reshape(v.shape[:-1] + (-1, 32))
    amax = np.abs(blocks).max(-1, keepdims=True)
    byte = np.maximum(np.where(amax > 0, np.frexp(amax)[1] - 1 + 127, 0) - down, 1)
    scale = np.exp2(byte - 127.0)
    codes = (blocks / scale).astype(np.float32).astype(dtype).astype(np.float64)
    return np.moveaxis((codes * scale).reshape(v.shape), -1, axis)


WIDE = False


def mx_kscale(k):
    if not WIDE:
        return np.ones(k)
    levels = np.array([10, -10, 5, -5, 0])
    if k % 512:
        return np.exp2(np.random.permutation(np.resize(levels, k // 32))).repeat(32)
    a = np.empty((k // 512, 16))
    for p in range(k // 512):
        a[p, :8] = np.random.permutation(np.resize(levels, 8))
        for g in range(8):
            far = levels[np.abs(levels - a[p, g]) >= 10]
            a[p, g + 8] = far[np.random.randint(len(far))]
    return np.exp2(a.ravel()).repeat(32)


def f64(x):
    return np.asarray(x).astype(np.float64)


def striped(idx):
    return np.tile(idx.reshape(-1, 16).T, (8, 1)).astype(np.uint16)


def unstriped(offs):
    return offs[:16].T.reshape(-1).astype(np.int64)


E2M1 = np.array([0.0, 0.5, 1.0, 1.5, 2.0, 3.0, 4.0, 6.0, -0.0, -0.5, -1.0, -1.5, -2.0, -3.0, -4.0, -6.0])


def pack_weight(w, fmt):
    k, n = w.shape
    w = f64(np.asarray(w, np.float32).astype(ml_dtypes.bfloat16)).reshape(k // 32, 32, n)
    amax = np.abs(w).max(1)
    if fmt == "e4m3":
        byte = np.frexp(amax)[1] - 1 + 127 - 7
    else:
        mant, ex = np.frexp(amax / 6.0)
        byte = np.where(mant > 0.5, ex, ex - 1) + 127
    byte = np.clip(np.where(amax > 0, byte, 1), 1, 254)
    scaled = (w * np.exp2(127.0 - byte)[:, None, :]).reshape(k, n).astype(np.float32)
    by_word = np.ascontiguousarray(scaled.reshape(k // 512, 128, 4, n).transpose(0, 1, 3, 2))
    if fmt == "e4m3":
        words = by_word.astype(ml_dtypes.float8_e4m3fn).view(np.uint8)
    else:
        c = by_word.astype(ml_dtypes.float4_e2m1fn).view(np.uint8) & 0xF
        words = (c[..., 0::2] | (c[..., 1::2] << 4)).reshape(k // 512, 128, 2 * n)
    return np.ascontiguousarray(words), np.ascontiguousarray(byte.astype(np.uint8).reshape(k // 512, 16, n))


def unpack_weight(words, scales, fmt):
    g, _, n = scales.shape
    words = np.ascontiguousarray(words).reshape(g, 128, n, -1)
    if fmt == "e4m3":
        vals = words.view(ml_dtypes.float8_e4m3fn).astype(np.float64)
    else:
        nib = np.empty((g, 128, n, 4), np.uint8)
        nib[..., 0::2] = words & 0xF
        nib[..., 1::2] = words >> 4
        vals = E2M1[nib]
    vals = vals * np.repeat(np.exp2(scales.astype(np.float64) - 127.0), 8, axis=1)[..., None]
    return vals.transpose(0, 1, 3, 2).reshape(g * 512, n)


def gelu(v):
    return 0.5 * v * (1.0 + np.tanh(np.sqrt(2.0 / np.pi) * (v + 0.044715 * v**3)))


def bf(x):
    return np.asarray(x, np.float32).astype(ml_dtypes.bfloat16)


def planes(Y):
    n, m = Y.shape
    b = f64(bf(Y)).reshape(n // 32, 32, m)
    amax = np.abs(b).max(1)
    byte = np.clip(np.where(amax > 0, np.frexp(amax)[1] - 1 + 127 - 7, 1), 1, 254)
    codes = (b * np.exp2(127.0 - byte)[:, None, :]).reshape(n, m).astype(np.float32).astype(ml_dtypes.float8_e4m3fn).view(np.uint8)
    words = codes.reshape(n // 512, 128, 4, m).transpose(0, 1, 3, 2)
    return np.ascontiguousarray(words), np.ascontiguousarray(byte.astype(np.uint8).reshape(n // 512, 16, m))


K, T, S, H, N, K2, T2, P = 1024, 4096, 1024, 512, 1024, 512, 2048, 512

def setup_inputs():
    n = np.random.standard_normal
    s, s2, u = mx_kscale(K)[:, None], mx_kscale(K2)[:, None], mx_kscale(H)[:, None]
    d = np.exp(0.8 * n(N))[None, :]
    tab_words, tab_scales = pack_weight(n((K, T)) * s, "e4m3")
    tab2_words, tab2_scales = pack_weight(n((K2, T2)) * s2, "e4m3")
    w1_words, w1_scales = pack_weight(n((K, H)) / np.sqrt(K) / s * u.T, "e2m1")
    wl_words, wl_scales = pack_weight(n((K2, N)) / np.sqrt(K2) / s2 * d, "e4m3")
    return {
        "tab_words": tab_words, "tab_scales": tab_scales,
        "offs": striped(np.random.permutation(T)[:S]),
        "tab2_words": tab2_words, "tab2_scales": tab2_scales,
        "offs2": striped(np.random.permutation(T2)[:P]),
        "pos1": striped(np.random.permutation(S)[:P]),
        "w1_words": w1_words, "w1_scales": w1_scales,
        "w2": (n((K, H)) / np.sqrt(K) / s * u.T).astype(np.float32),
        "w3": (0.52 * n((K, H)) / np.sqrt(K) / s).astype(np.float32),
        "gain": (np.random.uniform(2.5, 3.5, H) * u[:, 0]).astype(np.float32),
        "w4": (0.6 * n((H, N)) / np.sqrt(H) / u * d).astype(np.float32),
        "wl_words": wl_words, "wl_scales": wl_scales,
    }

def reference(tab_words, tab_scales, offs, tab2_words, tab2_scales, offs2, pos1,
              w1_words, w1_scales, w2, w3, gain, w4, wl_words, wl_scales):
    v = unpack_weight(tab_words, tab_scales, "e4m3")[:, unstriped(offs)]
    v2 = unpack_weight(tab2_words, tab2_scales, "e4m3")[:, unstriped(offs2)]
    a1 = unpack_weight(w1_words, w1_scales, "e2m1").T @ v
    a2 = mxq(f64(w2), 0, "e4m3").T @ v
    a3 = mxq(f64(w3), 0, "e4m3").T @ v
    h = np.maximum(a1, a2) + f64(gain)[:, None] * np.sin(a3)
    e = mxq(f64(w4), 0, "e4m3").T @ mxq(h, 0, "e4m3")
    b = unpack_weight(wl_words, wl_scales, "e4m3").T @ v2
    x = e[:, unstriped(pos1)]
    y = np.minimum(x, b) + x
    words, scales = planes(y)
    return y, words, scales

@@ -1,0 +1,300 @@
+from contextlib import ExitStack
+
+import concourse.mybir as mybir
+
+K, T, S, H, N, K2, T2, PICKS = 1024, 4096, 1024, 512, 1024, 512, 2048, 512
+FLOPS = 2 * (3 * K * H * S + H * N * S + K2 * N * PICKS)
+
+F32 = mybir.dt.float32
+BF16 = mybir.dt.bfloat16
+I32 = mybir.dt.int32
+U32 = mybir.dt.uint32
+U16 = mybir.dt.uint16
+U8 = mybir.dt.uint8
+FP8X4 = mybir.dt.float8_e4m3fn_x4
+FP4X4 = mybir.dt.float4_e2m1fn_x4
+ALU = mybir.AluOpType
+ACT = mybir.ActivationFunctionType
+
+P = 128
+PACK = 4
+PASS = P * PACK
+BANK = 512
+ALIGN = 64
+
+
+def tile_list_metaboliser_dosing_scores_kernel(
+    tc, tab_words, tab_scales, offs, tab2_words, tab2_scales, offs2, pos1,
+    w1_words, w1_scales, w2, w3, gain, w4, wl_words, wl_scales, out_0, out_1, out_2,
+):
+    nc = tc.nc
+    passes = K // PASS
+    halves = S // BANK
+    groups = N // PASS
+
+    with ExitStack() as ctx:
+        held = ctx.enter_context(tc.tile_pool(name="held", bufs=1))
+        ring = ctx.enter_context(tc.tile_pool(name="ring", bufs=3))
+        psum = ctx.enter_context(tc.psum_pool(name="psum", bufs=8))
+
+        def keep(shape, dtype, name):
+            return held.tile(shape, dtype, name=name, align_bytes=ALIGN)
+
+        idx = held.tile([P, S // 16], U16, name="idx")
+        idx2 = held.tile([P, PICKS // 16], U16, name="idx2")
+        pick = held.tile([P, PICKS // 16], U16, name="pick")
+        tab_rows = keep([P, T], U8, "tab_rows")
+        tab_w = [keep([P, T], U32, "tab_w%d" % a) for a in range(passes)]
+        tab2_w = keep([P, T2], U32, "tab2_w")
+        tab2_s = keep([P, T2], U8, "tab2_s")
+        w1_raw = keep([P, passes, 2 * H], U8, "w1_raw")
+        w1_raw_s = keep([P, passes, H], U8, "w1_raw_s")
+        wl_raw = keep([P, N], U32, "wl_raw")
+        wl_raw_s = keep([P, N], U8, "wl_raw_s")
+        v_s = keep([P, passes, S], U8, "v_s")
+        gain_sb = keep([P, PACK], F32, "gain_sb")
+
+        def flat(ap3):
+            return ap3.rearrange("p a c -> p (a c)")
+
+        nc.vector.memset(flat(w1_raw_s[:]).bitcast(I32), 0)
+        nc.vector.memset(tab_rows[32:64, :].bitcast(I32), 0)
+        nc.vector.memset(tab_rows[64:128, :].bitcast(I32), 0)
+        nc.vector.memset(flat(v_s[:]).bitcast(I32), 0)
+        nc.vector.memset(tab2_s[:].bitcast(I32), 0)
+        nc.vector.memset(wl_raw_s[:].bitcast(I32), 0)
+
+        def load_words(tile, words):
+            nc.sync.dma_start(out=tile[:].bitcast(I32), in_=words.rearrange("p t i -> p (t i)").bitcast(I32))
+
+        def load_weight(w, rows, cols, name):
+            raw = held.tile([P, PACK, BANK], F32, name=name)
+            nc.sync.dma_start(out=raw[:], in_=w[rows, cols].rearrange("(p j) c -> p j c", j=PACK))
+            return raw
+
+        nc.sync.dma_start(out=idx[:], in_=offs)
+        nc.sync.dma_start(
+            out=tab_rows[0:32, :].bitcast(I32), in_=tab_scales.rearrange("a q t -> (a q) t").bitcast(I32)
+        )
+        load_words(tab_w[0], tab_words[0])
+        nc.sync.dma_start(out=w1_raw[:].bitcast(I32), in_=w1_words.rearrange("a p b -> p a b").bitcast(I32))
+        load_words(tab_w[1], tab_words[1])
+        w2_raw = [load_weight(w2, slice(a * PASS, (a + 1) * PASS), slice(0, H), "w2_raw%d" % a) for a in range(passes)]
+        w3_raw = [load_weight(w3, slice(a * PASS, (a + 1) * PASS), slice(0, H), "w3_raw%d" % a) for a in range(passes)]
+        w4_raw = [load_weight(w4, slice(0, H), slice(0, PASS), "w4_raw0")]
+        nc.sync.dma_start(out=gain_sb[:], in_=gain.rearrange("(p t) -> p t", t=PACK))
+        nc.sync.dma_start(out=idx2[:], in_=offs2)
+        for q in range(4):
+            nc.sync.dma_start(
+                out=tab2_s[32 * q : 32 * q + 4, :].bitcast(I32), in_=tab2_scales[0, 4 * q : 4 * q + 4, :].bitcast(I32)
+            )
+        for q in range(4):
+            nc.sync.dma_start(
+                out=wl_raw_s[32 * q : 32 * q + 4, :].bitcast(I32), in_=wl_scales[0, 4 * q : 4 * q + 4, :].bitcast(I32)
+            )
+        load_words(tab2_w, tab2_words[0])
+        load_words(wl_raw, wl_words[0])
+        nc.sync.dma_start(out=pick[:], in_=pos1)
+        w4_raw.append(load_weight(w4, slice(0, H), slice(PASS, N), "w4_raw1"))
+
+        for q in range(4):
+            nc.gpsimd.dma_start(
+                out=w1_raw_s[32 * q : 32 * q + 4, :, :].bitcast(I32),
+                in_=w1_scales[:, 4 * q : 4 * q + 4, :].rearrange("a r c -> r a c").bitcast(I32),
+            )
+
+        v_rows = keep([P, S], U8, "v_rows")
+        nc.vector.tensor_copy(out=v_rows[:], in_=tab_rows[:].indirect(idx[:]))
+        for a in range(passes):
+            for q in range(4):
+                nc.gpsimd.dma_start(
+                    out=v_s[32 * q : 32 * q + 4, a, :].bitcast(I32),
+                    in_=v_rows[16 * a + 4 * q : 16 * a + 4 * q + 4, :].bitcast(I32),
+                )
+
+        def deal(dst, src):
+            nc.vector.tensor_copy(
+                out=dst.rearrange("p (g t m) -> p g m t", t=PACK, m=P),
+                in_=src.rearrange("p (g m t) -> p g m t", t=PACK, m=P),
+            )
+
+        w1_c = keep([P, passes, 2 * H], U8, "w1_c")
+        w1_s = keep([P, passes, H], U8, "w1_s")
+        deal(flat(w1_c[:]).bitcast(U16), flat(w1_raw[:]).bitcast(U16))
+        deal(flat(w1_s[:]), flat(w1_raw_s[:]))
+
+        cols16 = BANK // 16
+        v_c = [[keep([P, BANK], U32, "v_c%d_%d" % (a, u)) for u in range(halves)] for a in range(passes)]
+        for a in range(passes):
+            for u in range(halves):
+                nc.vector.tensor_copy(
+                    out=v_c[a][u][:], in_=tab_w[a][:].indirect(idx[:, u * cols16 : (u + 1) * cols16])
+                )
+
+        def copy_on(engine, out, in_):
+            if engine == "vector":
+                nc.vector.tensor_copy(out=out, in_=in_)
+            else:
+                nc.scalar.copy(out=out, in_=in_)
+
+        def round_weight(raw, engine):
+            grouped = ring.tile([P, PACK * BANK], BF16, name="grouped", tag="grouped", align_bytes=ALIGN)
+            dst = grouped[:].rearrange("p (t m j) -> p m j t", t=PACK, j=PACK)
+            src = raw[:].rearrange("p j (m t) -> p m j t", t=PACK)
+            for lo in (0, P // 2):
+                copy_on(engine, dst[:, lo : lo + P // 2], src[:, lo : lo + P // 2])
+            return grouped
+
+        def quantise(grouped, name):
+            codes = keep([P, BANK], U32, name + "_c")
+            scales = keep([P, BANK], U8, name + "_s")
+            nc.vector.quantize_mx(out=codes[:].bitcast(FP8X4), scales=scales[:], in_=grouped[:])
+            return codes, scales
+
+        def first_stage(weight_codes, weight_scales, t, u):
+            acc = psum.tile([P, BANK], F32, name="acc", tag="acc")
+            for a in range(passes):
+                nc.tensor.matmul_mx(
+                    out=acc[:], lhsT=weight_codes(a, t), lhsT_scale=weight_scales(a, t),
+                    rhs=v_c[a][u][:].bitcast(FP8X4), rhs_scale=v_s[:, a, u * BANK : (u + 1) * BANK],
+                    start=(a == 0), stop=(a == passes - 1),
+                )
+            return acc
+
+        def slices_of(quantised):
+            return (
+                lambda a, t: quantised[a][0][:, t * P : (t + 1) * P].bitcast(FP8X4),
+                lambda a, t: quantised[a][1][:, t * P : (t + 1) * P],
+            )
+
+        top = [held.tile([P, PACK, BANK], F32, name="top", tag="wide", bufs=2) for u in range(halves)]
+        for u in range(halves):
+            for t in range(PACK):
+                acc = first_stage(
+                    lambda a, t: w1_c[:, a, 2 * t * P : 2 * (t + 1) * P].bitcast(FP4X4),
+                    lambda a, t: w1_s[:, a, t * P : (t + 1) * P], t, u,
+                )
+                nc.scalar.copy(out=top[u][:, t, :], in_=acc[:])
+
+        w2_q = [quantise(round_weight(w2_raw[a], "vector"), "w2_%d" % a) for a in range(passes)]
+        w3_q = [quantise(round_weight(w3_raw[a], "scalar"), "w3_%d" % a) for a in range(passes)]
+
+        w2_codes, w2_planes = slices_of(w2_q)
+        for u in range(halves):
+            for t in range(PACK):
+                acc = first_stage(w2_codes, w2_planes, t, u)
+                nc.vector.tensor_tensor(out=top[u][:, t, :], in0=acc[:], in1=top[u][:, t, :], op=ALU.max)
+
+        def weave(dst, src, engine):
+            copy_on(
+                engine,
+                dst.rearrange("p (c i t) -> p c t i", i=4, t=PACK),
+                src.rearrange("p t (c i) -> p c t i", i=4),
+            )
+
+        w3_codes, w3_planes = slices_of(w3_q)
+        h_rows = []
+        for u in range(halves):
+            rows = held.tile([P, PACK, BANK], BF16, name="h_rows%d" % u)
+            for t in range(PACK):
+                acc = first_stage(w3_codes, w3_planes, t, u)
+                sine = ring.tile([P, BANK], F32, name="sine", tag="sine", bufs=4)
+                nc.scalar.activation(out=sine[:], in_=acc[:], func=ACT.Sin)
+                nc.vector.scalar_tensor_tensor(
+                    out=rows[:, t, :], in0=sine[:], scalar=gain_sb[:, t : t + 1], in1=top[u][:, t, :],
+                    op0=ALU.mult, op1=ALU.add,
+                )
+            h_rows.append(rows)
+        h_q = []
+        for u, engine in enumerate(("scalar", "vector")):
+            grouped = ring.tile([P, PACK * BANK], BF16, name="grouped", tag="grouped", align_bytes=ALIGN)
+            weave(grouped[:], h_rows[u][:], engine)
+            h_q.append(quantise(grouped, "h%d" % u))
+
+        w4_q = [quantise(round_weight(w4_raw[0], "scalar"), "w4_0")]
+
+        v2_c = keep([P, PICKS], U32, "v2_c")
+        v2_s = keep([P, PICKS], U8, "v2_s")
+        nc.vector.tensor_copy(out=v2_s[:], in_=tab2_s[:].indirect(idx2[:]))
+        nc.vector.tensor_copy(out=v2_c[:], in_=tab2_w[:].indirect(idx2[:]))
+        wl_c = keep([P, N], U32, "wl_c")
+        wl_s = keep([P, N], U8, "wl_s")
+        deal(wl_s[:], wl_raw_s[:])
+        deal(wl_c[:].bitcast(I32), wl_raw[:].bitcast(I32))
+
+        def scores(g, t):
+            e_rows = ring.tile([P, S], F32, name="e_rows", tag="e_rows", bufs=6)
+            codes, scales = w4_q[g]
+            for u in range(halves):
+                acc = psum.tile([P, BANK], F32, name="acc", tag="acc")
+                nc.tensor.matmul_mx(
+                    out=acc[:], lhsT=codes[:, t * P : (t + 1) * P].bitcast(FP8X4),
+                    lhsT_scale=scales[:, t * P : (t + 1) * P],
+                    rhs=h_q[u][0][:].bitcast(FP8X4), rhs_scale=h_q[u][1][:], start=True, stop=True,
+                )
+                nc.scalar.copy(out=e_rows[:, u * BANK : (u + 1) * BANK], in_=acc[:])
+            return e_rows
+
+        y = [held.tile([P, PACK, PICKS], F32, name="y", tag="wide", bufs=2) for g in range(groups)]
+        y_c = keep([P, groups, PICKS], U32, "y_c")
+        y_s = keep([P, groups, PICKS], U8, "y_s")
+
+        def fetch(e_rows, g, t, lo, hi):
+            x = ring.tile([P, hi - lo], F32, name="x", tag="x", bufs=4)
+            nc.vector.tensor_copy(out=x[:], in_=e_rows[:].indirect(pick[:, lo // 16 : hi // 16]))
+            acc = psum.tile([P, hi - lo], F32, name="acc", tag="acc")
+            n_cols = slice(g * PASS + t * P, g * PASS + (t + 1) * P)
+            nc.tensor.matmul_mx(
+                out=acc[:], lhsT=wl_c[:, n_cols].bitcast(FP8X4), lhsT_scale=wl_s[:, n_cols],
+                rhs=v2_c[:, lo:hi].bitcast(FP8X4), rhs_scale=v2_s[:, lo:hi], start=True, stop=True,
+            )
+            return x, acc
+
+        def lower(x, acc):
+            low = ring.tile(list(x.shape), F32, name="low", tag="low", bufs=3)
+            nc.vector.tensor_tensor(out=low[:], in0=acc[:], in1=x[:], op=ALU.min)
+            return low
+
+        def finish(x, low, g, t, lo, hi):
+            nc.vector.tensor_tensor(out=y[g][:, t, lo:hi], in0=low[:], in1=x[:], op=ALU.add)
+            rows = out_0[g * PASS : (g + 1) * PASS, :].rearrange("(p t) j -> p t j", t=PACK)
+            if hi - lo == PICKS:
+                nc.sync.dma_start(out=rows[:, t, :], in_=y[g][:, t, :])
+            elif t == PACK - 1:
+                nc.sync.dma_start(out=rows[:, :, lo:hi], in_=y[g][:, :, lo:hi])
+
+        def planes(g, lo, hi, engine):
+            grouped = ring.tile([P, PACK * (hi - lo)], BF16, name="grouped", tag="grouped", align_bytes=ALIGN)
+            weave(grouped[:], y[g][:, :, lo:hi], engine)
+            nc.vector.quantize_mx(out=y_c[:, g, lo:hi].bitcast(FP8X4), scales=y_s[:, g, lo:hi], in_=grouped[:])
+            nc.sync.dma_start(
+                out=out_1[g, :, lo:hi, :].rearrange("p m i -> p (m i)").bitcast(I32), in_=y_c[:, g, lo:hi].bitcast(I32)
+            )
+            if hi == PICKS:
+                for q in range(4):
+                    nc.sync.dma_start(
+                        out=out_2[g, 4 * q : 4 * q + 4, :].bitcast(I32),
+                        in_=y_s[32 * q : 32 * q + 4, g, :].bitcast(I32),
+                    )
+
+        half = PICKS // 2
+        steps = [(0, t, 0, PICKS) for t in range(PACK)]
+        steps.extend((1, t, lo, lo + half) for lo in (0, half) for t in range(PACK))
+        e_tiles = {}
+        fetched = {}
+        lowered = {}
+        for i in range(len(steps) + 2):
+            if i < len(steps):
+                g, t, lo, hi = steps[i]
+                if (g, t) == (1, 0) and lo == 0:
+                    w4_q.append(quantise(round_weight(w4_raw[1], "scalar"), "w4_1"))
+                if (g, t) not in e_tiles:
+                    e_tiles[(g, t)] = scores(g, t)
+                fetched[i] = fetch(e_tiles[(g, t)], g, t, lo, hi)
+            if 0 <= i - 1 < len(steps):
+                lowered[i - 1] = lower(*fetched[i - 1])
+            if 0 <= i - 2 < len(steps):
+                g, t, lo, hi = steps[i - 2]
+                finish(fetched[i - 2][0], lowered[i - 2], g, t, lo, hi)
+                if t == PACK - 1:
+                    planes(g, lo, hi, "vector" if i - 2 == len(steps) - 1 else "scalar")

@@ -35,7 +35,10 @@ def tile_list_metaboliser_dosing_scores_kernel(
     with ExitStack() as ctx:
         held = ctx.enter_context(tc.tile_pool(name="held", bufs=1))
         ring = ctx.enter_context(tc.tile_pool(name="ring", bufs=3))
-        psum = ctx.enter_context(tc.psum_pool(name="psum", bufs=8))
+        psum = ctx.enter_context(tc.psum_pool(name="psum", bufs=4))
+        stream = ctx.enter_context(tc.tile_pool(name="stream", bufs=1))
+        late = ctx.enter_context(tc.tile_pool(name="late", bufs=1))
+        place = PACK * BANK * 4
 
         def keep(shape, dtype, name):
             return held.tile(shape, dtype, name=name, align_bytes=ALIGN)
@@ -44,13 +47,9 @@ def tile_list_metaboliser_dosing_scores_kernel(
         idx2 = held.tile([P, PICKS // 16], U16, name="idx2")
         pick = held.tile([P, PICKS // 16], U16, name="pick")
         tab_rows = keep([P, T], U8, "tab_rows")
-        tab_w = [keep([P, T], U32, "tab_w%d" % a) for a in range(passes)]
-        tab2_w = keep([P, T2], U32, "tab2_w")
-        tab2_s = keep([P, T2], U8, "tab2_s")
+        tab_w = [stream.tile([P, T], U32, name="tab_w%d" % a, offset=2 * a * place) for a in range(passes)]
         w1_raw = keep([P, passes, 2 * H], U8, "w1_raw")
         w1_raw_s = keep([P, passes, H], U8, "w1_raw_s")
-        wl_raw = keep([P, N], U32, "wl_raw")
-        wl_raw_s = keep([P, N], U8, "wl_raw_s")
         v_s = keep([P, passes, S], U8, "v_s")
         gain_sb = keep([P, PACK], F32, "gain_sb")
 
@@ -61,14 +60,12 @@ def tile_list_metaboliser_dosing_scores_kernel(
         nc.vector.memset(tab_rows[32:64, :].bitcast(I32), 0)
         nc.vector.memset(tab_rows[64:128, :].bitcast(I32), 0)
         nc.vector.memset(flat(v_s[:]).bitcast(I32), 0)
-        nc.vector.memset(tab2_s[:].bitcast(I32), 0)
-        nc.vector.memset(wl_raw_s[:].bitcast(I32), 0)
 
         def load_words(tile, words):
             nc.sync.dma_start(out=tile[:].bitcast(I32), in_=words.rearrange("p t i -> p (t i)").bitcast(I32))
 
-        def load_weight(w, rows, cols, name):
-            raw = held.tile([P, PACK, BANK], F32, name=name)
+        def load_weight(w, rows, cols, name, at):
+            raw = stream.tile([P, PACK, BANK], F32, name=name, offset=at * place)
             nc.sync.dma_start(out=raw[:], in_=w[rows, cols].rearrange("(p j) c -> p j c", j=PACK))
             return raw
 
@@ -77,45 +74,38 @@ def tile_list_metaboliser_dosing_scores_kernel(
             out=tab_rows[0:32, :].bitcast(I32), in_=tab_scales.rearrange("a q t -> (a q) t").bitcast(I32)
         )
         load_words(tab_w[0], tab_words[0])
-        nc.sync.dma_start(out=w1_raw[:].bitcast(I32), in_=w1_words.rearrange("a p b -> p a b").bitcast(I32))
-        load_words(tab_w[1], tab_words[1])
-        w2_raw = [load_weight(w2, slice(a * PASS, (a + 1) * PASS), slice(0, H), "w2_raw%d" % a) for a in range(passes)]
-        w3_raw = [load_weight(w3, slice(a * PASS, (a + 1) * PASS), slice(0, H), "w3_raw%d" % a) for a in range(passes)]
-        w4_raw = [load_weight(w4, slice(0, H), slice(0, PASS), "w4_raw0")]
-        nc.sync.dma_start(out=gain_sb[:], in_=gain.rearrange("(p t) -> p t", t=PACK))
-        nc.sync.dma_start(out=idx2[:], in_=offs2)
         for q in range(4):
             nc.sync.dma_start(
-                out=tab2_s[32 * q : 32 * q + 4, :].bitcast(I32), in_=tab2_scales[0, 4 * q : 4 * q + 4, :].bitcast(I32)
-            )
-        for q in range(4):
-            nc.sync.dma_start(
-                out=wl_raw_s[32 * q : 32 * q + 4, :].bitcast(I32), in_=wl_scales[0, 4 * q : 4 * q + 4, :].bitcast(I32)
-            )
-        load_words(tab2_w, tab2_words[0])
-        load_words(wl_raw, wl_words[0])
-        nc.sync.dma_start(out=pick[:], in_=pos1)
-        w4_raw.append(load_weight(w4, slice(0, H), slice(PASS, N), "w4_raw1"))
-
-        for q in range(4):
-            nc.gpsimd.dma_start(
                 out=w1_raw_s[32 * q : 32 * q + 4, :, :].bitcast(I32),
                 in_=w1_scales[:, 4 * q : 4 * q + 4, :].rearrange("a r c -> r a c").bitcast(I32),
             )
+        nc.sync.dma_start(out=w1_raw[:].bitcast(I32), in_=w1_words.rearrange("a p b -> p a b").bitcast(I32))
+        load_words(tab_w[1], tab_words[1])
+        nc.sync.dma_start(out=idx2[:], in_=offs2)
+        nc.sync.dma_start(out=pick[:], in_=pos1)
 
         v_rows = keep([P, S], U8, "v_rows")
         nc.vector.tensor_copy(out=v_rows[:], in_=tab_rows[:].indirect(idx[:]))
-        for a in range(passes):
+        for a, queue in enumerate((nc.sync, nc.gpsimd)):
             for q in range(4):
-                nc.gpsimd.dma_start(
+                queue.dma_start(
                     out=v_s[32 * q : 32 * q + 4, a, :].bitcast(I32),
                     in_=v_rows[16 * a + 4 * q : 16 * a + 4 * q + 4, :].bitcast(I32),
                 )
 
-        def deal(dst, src):
-            nc.vector.tensor_copy(
-                out=dst.rearrange("p (g t m) -> p g m t", t=PACK, m=P),
-                in_=src.rearrange("p (g m t) -> p g m t", t=PACK, m=P),
+        nc.gpsimd.dma_start(out=gain_sb[:], in_=gain.rearrange("(p t) -> p t", t=PACK))
+
+        def copy_on(engine, out, in_):
+            if engine == "vector":
+                nc.vector.tensor_copy(out=out, in_=in_)
+            else:
+                nc.scalar.copy(out=out, in_=in_)
+
+        def deal(dst, src, engine="vector"):
+            copy_on(
+                engine,
+                dst.rearrange("p (g t m) -> p g m t", t=PACK, m=P),
+                src.rearrange("p (g m t) -> p g m t", t=PACK, m=P),
             )
 
         w1_c = keep([P, passes, 2 * H], U8, "w1_c")
@@ -131,28 +121,32 @@ def tile_list_metaboliser_dosing_scores_kernel(
                     out=v_c[a][u][:], in_=tab_w[a][:].indirect(idx[:, u * cols16 : (u + 1) * cols16])
                 )
 
-        def copy_on(engine, out, in_):
-            if engine == "vector":
-                nc.vector.tensor_copy(out=out, in_=in_)
-            else:
-                nc.scalar.copy(out=out, in_=in_)
+        w2_raw = [load_weight(w2, slice(a * PASS, (a + 1) * PASS), slice(0, H), "w2_raw%d" % a, a) for a in range(passes)]
+        w3_raw = [
+            load_weight(w3, slice(a * PASS, (a + 1) * PASS), slice(0, H), "w3_raw%d" % a, 2 + a) for a in range(passes)
+        ]
 
-        def round_weight(raw, engine):
-            grouped = ring.tile([P, PACK * BANK], BF16, name="grouped", tag="grouped", align_bytes=ALIGN)
+        def rounded_tile(width, tag):
+            return ring.tile([P, width], BF16, name="grouped", tag=tag, bufs={"early": 3, "late": 2}[tag], align_bytes=ALIGN)
+
+        def round_weight(raw, engines, grouped):
             dst = grouped[:].rearrange("p (t m j) -> p m j t", t=PACK, j=PACK)
             src = raw[:].rearrange("p j (m t) -> p m j t", t=PACK)
-            for lo in (0, P // 2):
+            for lo, engine in zip((0, P // 2), engines):
                 copy_on(engine, dst[:, lo : lo + P // 2], src[:, lo : lo + P // 2])
             return grouped
 
-        def quantise(grouped, name):
-            codes = keep([P, BANK], U32, name + "_c")
+        def placed(shape, dtype, name, unit, extra=0):
+            return late.tile(shape, dtype, name=name, offset=unit * 4 * BANK + extra, align_bytes=ALIGN)
+
+        def quantise(grouped, name, unit=None):
+            codes = keep([P, BANK], U32, name + "_c") if unit is None else placed([P, BANK], U32, name + "_c", unit)
             scales = keep([P, BANK], U8, name + "_s")
             nc.vector.quantize_mx(out=codes[:].bitcast(FP8X4), scales=scales[:], in_=grouped[:])
             return codes, scales
 
-        def first_stage(weight_codes, weight_scales, t, u):
-            acc = psum.tile([P, BANK], F32, name="acc", tag="acc")
+        def first_stage(weight_codes, weight_scales, t, u, banks):
+            acc = psum.tile([P, BANK], F32, name="acc", tag=banks)
             for a in range(passes):
                 nc.tensor.matmul_mx(
                     out=acc[:], lhsT=weight_codes(a, t), lhsT_scale=weight_scales(a, t),
@@ -167,22 +161,45 @@ def tile_list_metaboliser_dosing_scores_kernel(
                 lambda a, t: quantised[a][1][:, t * P : (t + 1) * P],
             )
 
+        w2_q = [
+            quantise(round_weight(w2_raw[a], engines, rounded_tile(PACK * BANK, "early")), "w2_%d" % a)
+            for a, engines in enumerate((("vector", "vector"), ("vector", "scalar")))
+        ]
+
         top = [held.tile([P, PACK, BANK], F32, name="top", tag="wide", bufs=2) for u in range(halves)]
         for u in range(halves):
             for t in range(PACK):
                 acc = first_stage(
                     lambda a, t: w1_c[:, a, 2 * t * P : 2 * (t + 1) * P].bitcast(FP4X4),
-                    lambda a, t: w1_s[:, a, t * P : (t + 1) * P], t, u,
+                    lambda a, t: w1_s[:, a, t * P : (t + 1) * P], t, u, "scalar_banks",
                 )
                 nc.scalar.copy(out=top[u][:, t, :], in_=acc[:])
 
-        w2_q = [quantise(round_weight(w2_raw[a], "vector"), "w2_%d" % a) for a in range(passes)]
-        w3_q = [quantise(round_weight(w3_raw[a], "scalar"), "w3_%d" % a) for a in range(passes)]
+        w3_q = [quantise(round_weight(w3_raw[a], ("scalar", "scalar"), rounded_tile(PACK * BANK, "early")), "w3_%d" % a) for a in range(passes)]
+
+        w4_raw = [load_weight(w4, slice(0, H), slice(0, PASS), "w4_raw0", 0)]
+        wl_raw = stream.tile([P, N], U32, name="wl_raw", offset=place)
+        wl_raw_s = stream.tile([P, N], U8, name="wl_raw_s", offset=place + 4 * N)
+        tab2_s = stream.tile([P, T2], U8, name="tab2_s", offset=place + 5 * N)
+        load_words(wl_raw, wl_words[0])
+        nc.gpsimd.memset(tab2_s[:].bitcast(I32), 0)
+        nc.gpsimd.memset(wl_raw_s[:].bitcast(I32), 0)
+        for q in range(4):
+            nc.sync.dma_start(
+                out=tab2_s[32 * q : 32 * q + 4, :].bitcast(I32), in_=tab2_scales[0, 4 * q : 4 * q + 4, :].bitcast(I32)
+            )
+        for q in range(4):
+            nc.sync.dma_start(
+                out=wl_raw_s[32 * q : 32 * q + 4, :].bitcast(I32), in_=wl_scales[0, 4 * q : 4 * q + 4, :].bitcast(I32)
+            )
+        tab2_w = stream.tile([P, T2], U32, name="tab2_w", offset=2 * place)
+        load_words(tab2_w, tab2_words[0])
+        w4_raw.append(load_weight(w4, slice(0, H), slice(PASS, N), "w4_raw1", 3))
 
         w2_codes, w2_planes = slices_of(w2_q)
         for u in range(halves):
             for t in range(PACK):
-                acc = first_stage(w2_codes, w2_planes, t, u)
+                acc = first_stage(w2_codes, w2_planes, t, u, "vector_banks")
                 nc.vector.tensor_tensor(out=top[u][:, t, :], in0=acc[:], in1=top[u][:, t, :], op=ALU.max)
 
         def weave(dst, src, engine):
@@ -195,10 +212,10 @@ def tile_list_metaboliser_dosing_scores_kernel(
         w3_codes, w3_planes = slices_of(w3_q)
         h_rows = []
         for u in range(halves):
-            rows = held.tile([P, PACK, BANK], BF16, name="h_rows%d" % u)
+            rows = placed([P, PACK, BANK], BF16, "h_rows%d" % u, 8 + 2 * u)
             for t in range(PACK):
-                acc = first_stage(w3_codes, w3_planes, t, u)
-                sine = ring.tile([P, BANK], F32, name="sine", tag="sine", bufs=4)
+                acc = first_stage(w3_codes, w3_planes, t, u, ("scalar_banks", "vector_banks")[u])
+                sine = placed([P, BANK], F32, "sine%d_%d" % (u, t), PACK * u + t)
                 nc.scalar.activation(out=sine[:], in_=acc[:], func=ACT.Sin)
                 nc.vector.scalar_tensor_tensor(
                     out=rows[:, t, :], in0=sine[:], scalar=gain_sb[:, t : t + 1], in1=top[u][:, t, :],
@@ -207,26 +224,26 @@ def tile_list_metaboliser_dosing_scores_kernel(
             h_rows.append(rows)
         h_q = []
         for u, engine in enumerate(("scalar", "vector")):
-            grouped = ring.tile([P, PACK * BANK], BF16, name="grouped", tag="grouped", align_bytes=ALIGN)
+            grouped = rounded_tile(PACK * BANK, "late")
             weave(grouped[:], h_rows[u][:], engine)
-            h_q.append(quantise(grouped, "h%d" % u))
+            h_q.append(quantise(grouped, "h%d" % u, 12 + u))
 
-        w4_q = [quantise(round_weight(w4_raw[0], "scalar"), "w4_0")]
+        w4_q = [quantise(round_weight(w4_raw[0], ("scalar", "scalar"), rounded_tile(PACK * BANK, "early")), "w4_0")]
 
-        v2_c = keep([P, PICKS], U32, "v2_c")
-        v2_s = keep([P, PICKS], U8, "v2_s")
+        v2_c = placed([P, PICKS], U32, "v2_c", 10)
+        v2_s = placed([P, PICKS], U8, "v2_s", 11)
         nc.vector.tensor_copy(out=v2_s[:], in_=tab2_s[:].indirect(idx2[:]))
         nc.vector.tensor_copy(out=v2_c[:], in_=tab2_w[:].indirect(idx2[:]))
-        wl_c = keep([P, N], U32, "wl_c")
-        wl_s = keep([P, N], U8, "wl_s")
+        wl_c = placed([P, N], U32, "wl_c", 2)
+        wl_s = placed([P, N], U8, "wl_s", 11, PICKS)
         deal(wl_s[:], wl_raw_s[:])
-        deal(wl_c[:].bitcast(I32), wl_raw[:].bitcast(I32))
+        deal(wl_c[:], wl_raw[:], "scalar")
 
         def scores(g, t):
-            e_rows = ring.tile([P, S], F32, name="e_rows", tag="e_rows", bufs=6)
+            e_rows = ring.tile([P, S], F32, name="e_rows", tag="e_rows", bufs=8)
             codes, scales = w4_q[g]
             for u in range(halves):
-                acc = psum.tile([P, BANK], F32, name="acc", tag="acc")
+                acc = psum.tile([P, BANK], F32, name="acc", tag="scalar_banks")
                 nc.tensor.matmul_mx(
                     out=acc[:], lhsT=codes[:, t * P : (t + 1) * P].bitcast(FP8X4),
                     lhsT_scale=scales[:, t * P : (t + 1) * P],
@@ -239,32 +256,23 @@ def tile_list_metaboliser_dosing_scores_kernel(
         y_c = keep([P, groups, PICKS], U32, "y_c")
         y_s = keep([P, groups, PICKS], U8, "y_s")
 
-        def fetch(e_rows, g, t, lo, hi):
-            x = ring.tile([P, hi - lo], F32, name="x", tag="x", bufs=4)
-            nc.vector.tensor_copy(out=x[:], in_=e_rows[:].indirect(pick[:, lo // 16 : hi // 16]))
-            acc = psum.tile([P, hi - lo], F32, name="acc", tag="acc")
+        def level_scores(g, t):
+            acc = psum.tile([P, PICKS], F32, name="acc", tag="vector_banks")
             n_cols = slice(g * PASS + t * P, g * PASS + (t + 1) * P)
             nc.tensor.matmul_mx(
                 out=acc[:], lhsT=wl_c[:, n_cols].bitcast(FP8X4), lhsT_scale=wl_s[:, n_cols],
-                rhs=v2_c[:, lo:hi].bitcast(FP8X4), rhs_scale=v2_s[:, lo:hi], start=True, stop=True,
+                rhs=v2_c[:].bitcast(FP8X4), rhs_scale=v2_s[:], start=True, stop=True,
             )
-            return x, acc
+            return acc
 
-        def lower(x, acc):
-            low = ring.tile(list(x.shape), F32, name="low", tag="low", bufs=3)
-            nc.vector.tensor_tensor(out=low[:], in0=acc[:], in1=x[:], op=ALU.min)
-            return low
-
-        def finish(x, low, g, t, lo, hi):
-            nc.vector.tensor_tensor(out=y[g][:, t, lo:hi], in0=low[:], in1=x[:], op=ALU.add)
+        def finish(g, t, lo, hi, adder):
+            x, low = picked[(g, t)], lowered[(g, t)]
+            adder.tensor_tensor(out=y[g][:, t, lo:hi], in0=low[:, lo:hi], in1=x[:, lo:hi], op=ALU.add)
             rows = out_0[g * PASS : (g + 1) * PASS, :].rearrange("(p t) j -> p t j", t=PACK)
-            if hi - lo == PICKS:
-                nc.sync.dma_start(out=rows[:, t, :], in_=y[g][:, t, :])
-            elif t == PACK - 1:
-                nc.sync.dma_start(out=rows[:, :, lo:hi], in_=y[g][:, :, lo:hi])
+            nc.sync.dma_start(out=rows[:, t, lo:hi], in_=y[g][:, t, lo:hi])
 
         def planes(g, lo, hi, engine):
-            grouped = ring.tile([P, PACK * (hi - lo)], BF16, name="grouped", tag="grouped", align_bytes=ALIGN)
+            grouped = placed([P, PACK * PICKS], BF16, "y0_rounded", 12) if g == 0 else rounded_tile(PACK * (hi - lo), "late")
             weave(grouped[:], y[g][:, :, lo:hi], engine)
             nc.vector.quantize_mx(out=y_c[:, g, lo:hi].bitcast(FP8X4), scales=y_s[:, g, lo:hi], in_=grouped[:])
             nc.sync.dma_start(
@@ -278,23 +286,36 @@ def tile_list_metaboliser_dosing_scores_kernel(
                     )
 
         half = PICKS // 2
-        steps = [(0, t, 0, PICKS) for t in range(PACK)]
-        steps.extend((1, t, lo, lo + half) for lo in (0, half) for t in range(PACK))
-        e_tiles = {}
-        fetched = {}
-        lowered = {}
-        for i in range(len(steps) + 2):
-            if i < len(steps):
-                g, t, lo, hi = steps[i]
-                if (g, t) == (1, 0) and lo == 0:
-                    w4_q.append(quantise(round_weight(w4_raw[1], "scalar"), "w4_1"))
-                if (g, t) not in e_tiles:
-                    e_tiles[(g, t)] = scores(g, t)
-                fetched[i] = fetch(e_tiles[(g, t)], g, t, lo, hi)
-            if 0 <= i - 1 < len(steps):
-                lowered[i - 1] = lower(*fetched[i - 1])
-            if 0 <= i - 2 < len(steps):
-                g, t, lo, hi = steps[i - 2]
-                finish(fetched[i - 2][0], lowered[i - 2], g, t, lo, hi)
-                if t == PACK - 1:
-                    planes(g, lo, hi, "vector" if i - 2 == len(steps) - 1 else "scalar")
+        e_tiles = {(0, t): scores(0, t) for t in range(PACK)}
+        w4_q.append(quantise(round_weight(w4_raw[1], ("scalar", "scalar"), placed([P, PACK * BANK], BF16, "w4_1_rounded", 8)), "w4_1"))
+        for t in range(PACK):
+            e_tiles[(1, t)] = scores(1, t)
+
+        picked, lowered, levels = {}, {}, {}
+
+        def pair(pieces):
+            for g, t, lo in pieces:
+                if (g, t) not in picked:
+                    picked[(g, t)] = ring.tile([P, PICKS], F32, name="picked", tag="picked", bufs=4)
+                    lowered[(g, t)] = ring.tile([P, PICKS], F32, name="lowered", tag="lowered", bufs=4)
+                    levels[(g, t)] = level_scores(g, t)
+                nc.vector.tensor_copy(
+                    out=picked[(g, t)][:, lo : lo + half],
+                    in_=e_tiles[(g, t)][:].indirect(pick[:, lo // 16 : (lo + half) // 16]),
+                )
+            for g, t, lo in pieces:
+                cols = slice(lo, lo + half)
+                nc.vector.tensor_tensor(
+                    out=lowered[(g, t)][:, cols], in0=levels[(g, t)][:, cols], in1=picked[(g, t)][:, cols], op=ALU.min
+                )
+
+        for g, t in [(0, 0), (0, 1), (0, 2), (0, 3), (1, 0), (1, 1)]:
+            pair([(g, t, 0), (g, t, half)])
+            finish(g, t, 0, PICKS, nc.gpsimd)
+            if (g, t) == (0, PACK - 1):
+                planes(0, 0, PICKS, "scalar")
+        for lo, adder, weaver in ((0, nc.gpsimd, "scalar"), (half, nc.vector, "vector")):
+            pair([(1, 2, lo), (1, 3, lo)])
+            for t in (2, 3):
+                finish(1, t, lo, lo + half, adder)
+            planes(1, lo, lo + half, weaver)

@@ -162,8 +162,8 @@ def tile_list_metaboliser_dosing_scores_kernel(
             )
 
         w2_q = [
-            quantise(round_weight(w2_raw[a], engines, rounded_tile(PACK * BANK, "early")), "w2_%d" % a)
-            for a, engines in enumerate((("vector", "vector"), ("vector", "scalar")))
+            quantise(round_weight(w2_raw[a], ("vector", "vector"), rounded_tile(PACK * BANK, "early")), "w2_%d" % a)
+            for a in range(passes)
         ]
 
         top = [held.tile([P, PACK, BANK], F32, name="top", tag="wide", bufs=2) for u in range(halves)]
@@ -224,20 +224,20 @@ def tile_list_metaboliser_dosing_scores_kernel(
             h_rows.append(rows)
         h_q = []
         for u, engine in enumerate(("scalar", "vector")):
-            grouped = rounded_tile(PACK * BANK, "late")
+            grouped = placed([P, PACK * BANK], BF16, "h_rounded%d" % u, 14 + 2 * u)
             weave(grouped[:], h_rows[u][:], engine)
             h_q.append(quantise(grouped, "h%d" % u, 12 + u))
 
         w4_q = [quantise(round_weight(w4_raw[0], ("scalar", "scalar"), rounded_tile(PACK * BANK, "early")), "w4_0")]
 
-        v2_c = placed([P, PICKS], U32, "v2_c", 10)
-        v2_s = placed([P, PICKS], U8, "v2_s", 11)
+        v2_c = placed([P, PICKS], U32, "v2_c", 16)
+        v2_s = placed([P, PICKS], U8, "v2_s", 17)
         nc.vector.tensor_copy(out=v2_s[:], in_=tab2_s[:].indirect(idx2[:]))
         nc.vector.tensor_copy(out=v2_c[:], in_=tab2_w[:].indirect(idx2[:]))
         wl_c = placed([P, N], U32, "wl_c", 2)
-        wl_s = placed([P, N], U8, "wl_s", 11, PICKS)
+        wl_s = placed([P, N], U8, "wl_s", 17, PICKS)
         deal(wl_s[:], wl_raw_s[:])
-        deal(wl_c[:], wl_raw[:], "scalar")
+        deal(wl_c[:, 0:PASS], wl_raw[:, 0:PASS], "scalar")
 
         def scores(g, t):
             e_rows = ring.tile([P, S], F32, name="e_rows", tag="e_rows", bufs=8)
@@ -280,16 +280,17 @@ def tile_list_metaboliser_dosing_scores_kernel(
             )
             if hi == PICKS:
                 for q in range(4):
-                    nc.sync.dma_start(
+                    (nc.sync, nc.scalar)[g * (q % 2)].dma_start(
                         out=out_2[g, 4 * q : 4 * q + 4, :].bitcast(I32),
                         in_=y_s[32 * q : 32 * q + 4, g, :].bitcast(I32),
                     )
 
         half = PICKS // 2
-        e_tiles = {(0, t): scores(0, t) for t in range(PACK)}
-        w4_q.append(quantise(round_weight(w4_raw[1], ("scalar", "scalar"), placed([P, PACK * BANK], BF16, "w4_1_rounded", 8)), "w4_1"))
-        for t in range(PACK):
-            e_tiles[(1, t)] = scores(1, t)
+        e_tiles = {(0, t): scores(0, t) for t in range(2)}
+        w4_q.append(quantise(round_weight(w4_raw[1], ("scalar", "scalar"), placed([P, PACK * BANK], BF16, "w4_1_rounded", 10)), "w4_1"))
+        deal(wl_c[:, PASS:N], wl_raw[:, PASS:N], "scalar")
+        for g, t in [(0, 2), (0, 3), (1, 0), (1, 1), (1, 2), (1, 3)]:
+            e_tiles[(g, t)] = scores(g, t)
 
         picked, lowered, levels = {}, {}, {}
 

@@ -98,6 +98,8 @@ def tile_list_metaboliser_dosing_scores_kernel(
         def copy_on(engine, out, in_):
             if engine == "vector":
                 nc.vector.tensor_copy(out=out, in_=in_)
+            elif engine == "gpsimd":
+                nc.gpsimd.tensor_scalar(out=out, in0=in_, scalar1=1.0, scalar2=0.0, op0=ALU.mult, op1=ALU.add)
             else:
                 nc.scalar.copy(out=out, in_=in_)
 
@@ -130,10 +132,12 @@ def tile_list_metaboliser_dosing_scores_kernel(
             return ring.tile([P, width], BF16, name="grouped", tag=tag, bufs={"early": 3, "late": 2}[tag], align_bytes=ALIGN)
 
         def round_weight(raw, engines, grouped):
-            dst = grouped[:].rearrange("p (t m j) -> p m j t", t=PACK, j=PACK)
-            src = raw[:].rearrange("p j (m t) -> p m j t", t=PACK)
-            for lo, engine in zip((0, P // 2), engines):
-                copy_on(engine, dst[:, lo : lo + P // 2], src[:, lo : lo + P // 2])
+            walk = "p m t j" if engines[0] == "gpsimd" else "p m j t"
+            dst = grouped[:].rearrange("p (t m j) -> " + walk, t=PACK, j=PACK)
+            src = raw[:].rearrange("p j (m t) -> " + walk, t=PACK)
+            share = P // len(engines)
+            for i, engine in enumerate(engines):
+                copy_on(engine, dst[:, i * share : (i + 1) * share], src[:, i * share : (i + 1) * share])
             return grouped
 
         def placed(shape, dtype, name, unit, extra=0):
@@ -223,12 +227,14 @@ def tile_list_metaboliser_dosing_scores_kernel(
                 )
             h_rows.append(rows)
         h_q = []
-        for u, engine in enumerate(("scalar", "vector")):
+        for u, engines in enumerate((("scalar", "scalar"), ("scalar", "vector"))):
             grouped = placed([P, PACK * BANK], BF16, "h_rounded%d" % u, 14 + 2 * u)
-            weave(grouped[:], h_rows[u][:], engine)
+            for i, engine in enumerate(engines):
+                lo, hi = i * BANK // 2, (i + 1) * BANK // 2
+                weave(grouped[:, PACK * lo : PACK * hi], h_rows[u][:, :, lo:hi], engine)
             h_q.append(quantise(grouped, "h%d" % u, 12 + u))
 
-        w4_q = [quantise(round_weight(w4_raw[0], ("scalar", "scalar"), rounded_tile(PACK * BANK, "early")), "w4_0")]
+        w4_q = [quantise(round_weight(w4_raw[0], ("gpsimd",) * 4, rounded_tile(PACK * BANK, "early")), "w4_0")]
 
         v2_c = placed([P, PICKS], U32, "v2_c", 16)
         v2_s = placed([P, PICKS], U8, "v2_s", 17)
@@ -236,7 +242,10 @@ def tile_list_metaboliser_dosing_scores_kernel(
         nc.vector.tensor_copy(out=v2_c[:], in_=tab2_w[:].indirect(idx2[:]))
         wl_c = placed([P, N], U32, "wl_c", 2)
         wl_s = placed([P, N], U8, "wl_s", 17, PICKS)
-        deal(wl_s[:], wl_raw_s[:])
+        for g in range(groups):
+            by_slice = wl_raw_s[:, g * PASS : (g + 1) * PASS].rearrange("p (m t) -> p t m", t=PACK)
+            for t in range(PACK):
+                nc.gpsimd.tensor_copy(out=wl_s[:, g * PASS + t * P : g * PASS + (t + 1) * P], in_=by_slice[:, t, :])
         deal(wl_c[:, 0:PASS], wl_raw[:, 0:PASS], "scalar")
 
         def scores(g, t):

from contextlib import ExitStack

import concourse.mybir as mybir

K, T, S, H, N, K2, T2, PICKS = 1024, 4096, 1024, 512, 1024, 512, 2048, 512
FLOPS = 2 * (3 * K * H * S + H * N * S + K2 * N * PICKS)

F32 = mybir.dt.float32
BF16 = mybir.dt.bfloat16
I32 = mybir.dt.int32
U32 = mybir.dt.uint32
U16 = mybir.dt.uint16
U8 = mybir.dt.uint8
FP8X4 = mybir.dt.float8_e4m3fn_x4
FP4X4 = mybir.dt.float4_e2m1fn_x4
ALU = mybir.AluOpType
ACT = mybir.ActivationFunctionType

P = 128
PACK = 4
PASS = P * PACK
BANK = 512
ALIGN = 64


def tile_list_metaboliser_dosing_scores_kernel(
    tc, tab_words, tab_scales, offs, tab2_words, tab2_scales, offs2, pos1,
    w1_words, w1_scales, w2, w3, gain, w4, wl_words, wl_scales, out_0, out_1, out_2,
):
    nc = tc.nc
    passes = K // PASS
    halves = S // BANK
    groups = N // PASS

    with ExitStack() as ctx:
        held = ctx.enter_context(tc.tile_pool(name="held", bufs=1))
        ring = ctx.enter_context(tc.tile_pool(name="ring", bufs=3))
        psum = ctx.enter_context(tc.psum_pool(name="psum", bufs=4))
        stream = ctx.enter_context(tc.tile_pool(name="stream", bufs=1))
        late = ctx.enter_context(tc.tile_pool(name="late", bufs=1))
        place = PACK * BANK * 4

        def keep(shape, dtype, name):
            return held.tile(shape, dtype, name=name, align_bytes=ALIGN)

        idx = held.tile([P, S // 16], U16, name="idx")
        idx2 = held.tile([P, PICKS // 16], U16, name="idx2")
        pick = held.tile([P, PICKS // 16], U16, name="pick")
        tab_rows = keep([P, T], U8, "tab_rows")
        tab_w = [stream.tile([P, T], U32, name="tab_w%d" % a, offset=2 * a * place) for a in range(passes)]
        w1_raw = keep([P, passes, 2 * H], U8, "w1_raw")
        w1_raw_s = keep([P, passes, H], U8, "w1_raw_s")
        v_s = keep([P, passes, S], U8, "v_s")
        gain_sb = keep([P, PACK], F32, "gain_sb")

        def flat(ap3):
            return ap3.rearrange("p a c -> p (a c)")

        nc.vector.memset(flat(w1_raw_s[:]).bitcast(I32), 0)
        nc.vector.memset(tab_rows[32:64, :].bitcast(I32), 0)
        nc.vector.memset(tab_rows[64:128, :].bitcast(I32), 0)
        nc.vector.memset(flat(v_s[:]).bitcast(I32), 0)

        def load_words(tile, words):
            nc.sync.dma_start(out=tile[:].bitcast(I32), in_=words.rearrange("p t i -> p (t i)").bitcast(I32))

        def load_weight(w, rows, cols, name, at):
            raw = stream.tile([P, PACK, BANK], F32, name=name, offset=at * place)
            nc.sync.dma_start(out=raw[:], in_=w[rows, cols].rearrange("(p j) c -> p j c", j=PACK))
            return raw

        nc.sync.dma_start(out=idx[:], in_=offs)
        nc.sync.dma_start(
            out=tab_rows[0:32, :].bitcast(I32), in_=tab_scales.rearrange("a q t -> (a q) t").bitcast(I32)
        )
        load_words(tab_w[0], tab_words[0])
        for q in range(4):
            nc.sync.dma_start(
                out=w1_raw_s[32 * q : 32 * q + 4, :, :].bitcast(I32),
                in_=w1_scales[:, 4 * q : 4 * q + 4, :].rearrange("a r c -> r a c").bitcast(I32),
            )
        nc.sync.dma_start(out=w1_raw[:].bitcast(I32), in_=w1_words.rearrange("a p b -> p a b").bitcast(I32))
        load_words(tab_w[1], tab_words[1])
        nc.sync.dma_start(out=idx2[:], in_=offs2)
        nc.sync.dma_start(out=pick[:], in_=pos1)

        v_rows = keep([P, S], U8, "v_rows")
        nc.vector.tensor_copy(out=v_rows[:], in_=tab_rows[:].indirect(idx[:]))
        for a, queue in enumerate((nc.sync, nc.gpsimd)):
            for q in range(4):
                queue.dma_start(
                    out=v_s[32 * q : 32 * q + 4, a, :].bitcast(I32),
                    in_=v_rows[16 * a + 4 * q : 16 * a + 4 * q + 4, :].bitcast(I32),
                )

        nc.gpsimd.dma_start(out=gain_sb[:], in_=gain.rearrange("(p t) -> p t", t=PACK))

        def copy_on(engine, out, in_):
            if engine == "vector":
                nc.vector.tensor_copy(out=out, in_=in_)
            elif engine == "gpsimd":
                nc.gpsimd.tensor_scalar(out=out, in0=in_, scalar1=1.0, scalar2=0.0, op0=ALU.mult, op1=ALU.add)
            else:
                nc.scalar.copy(out=out, in_=in_)

        def deal(dst, src, engine="vector"):
            copy_on(
                engine,
                dst.rearrange("p (g t m) -> p g m t", t=PACK, m=P),
                src.rearrange("p (g m t) -> p g m t", t=PACK, m=P),
            )

        w1_c = keep([P, passes, 2 * H], U8, "w1_c")
        w1_s = keep([P, passes, H], U8, "w1_s")
        deal(flat(w1_c[:]).bitcast(U16), flat(w1_raw[:]).bitcast(U16))
        deal(flat(w1_s[:]), flat(w1_raw_s[:]))

        cols16 = BANK // 16
        v_c = [[keep([P, BANK], U32, "v_c%d_%d" % (a, u)) for u in range(halves)] for a in range(passes)]
        for a in range(passes):
            for u in range(halves):
                nc.vector.tensor_copy(
                    out=v_c[a][u][:], in_=tab_w[a][:].indirect(idx[:, u * cols16 : (u + 1) * cols16])
                )

        w2_raw = [load_weight(w2, slice(a * PASS, (a + 1) * PASS), slice(0, H), "w2_raw%d" % a, a) for a in range(passes)]
        w3_raw = [
            load_weight(w3, slice(a * PASS, (a + 1) * PASS), slice(0, H), "w3_raw%d" % a, 2 + a) for a in range(passes)
        ]

        def rounded_tile(width, tag):
            return ring.tile([P, width], BF16, name="grouped", tag=tag, bufs={"early": 3, "late": 2}[tag], align_bytes=ALIGN)

        def round_weight(raw, engines, grouped):
            walk = "p m t j" if engines[0] == "gpsimd" else "p m j t"
            dst = grouped[:].rearrange("p (t m j) -> " + walk, t=PACK, j=PACK)
            src = raw[:].rearrange("p j (m t) -> " + walk, t=PACK)
            share = P // len(engines)
            for i, engine in enumerate(engines):
                copy_on(engine, dst[:, i * share : (i + 1) * share], src[:, i * share : (i + 1) * share])
            return grouped

        def placed(shape, dtype, name, unit, extra=0):
            return late.tile(shape, dtype, name=name, offset=unit * 4 * BANK + extra, align_bytes=ALIGN)

        def quantise(grouped, name, unit=None):
            codes = keep([P, BANK], U32, name + "_c") if unit is None else placed([P, BANK], U32, name + "_c", unit)
            scales = keep([P, BANK], U8, name + "_s")
            nc.vector.quantize_mx(out=codes[:].bitcast(FP8X4), scales=scales[:], in_=grouped[:])
            return codes, scales

        def first_stage(weight_codes, weight_scales, t, u, banks):
            acc = psum.tile([P, BANK], F32, name="acc", tag=banks)
            for a in range(passes):
                nc.tensor.matmul_mx(
                    out=acc[:], lhsT=weight_codes(a, t), lhsT_scale=weight_scales(a, t),
                    rhs=v_c[a][u][:].bitcast(FP8X4), rhs_scale=v_s[:, a, u * BANK : (u + 1) * BANK],
                    start=(a == 0), stop=(a == passes - 1),
                )
            return acc

        def slices_of(quantised):
            return (
                lambda a, t: quantised[a][0][:, t * P : (t + 1) * P].bitcast(FP8X4),
                lambda a, t: quantised[a][1][:, t * P : (t + 1) * P],
            )

        w2_q = [
            quantise(round_weight(w2_raw[a], ("vector", "vector"), rounded_tile(PACK * BANK, "early")), "w2_%d" % a)
            for a in range(passes)
        ]

        top = [held.tile([P, PACK, BANK], F32, name="top", tag="wide", bufs=2) for u in range(halves)]
        for u in range(halves):
            for t in range(PACK):
                acc = first_stage(
                    lambda a, t: w1_c[:, a, 2 * t * P : 2 * (t + 1) * P].bitcast(FP4X4),
                    lambda a, t: w1_s[:, a, t * P : (t + 1) * P], t, u, "scalar_banks",
                )
                nc.scalar.copy(out=top[u][:, t, :], in_=acc[:])

        w3_q = [quantise(round_weight(w3_raw[a], ("scalar", "scalar"), rounded_tile(PACK * BANK, "early")), "w3_%d" % a) for a in range(passes)]

        w4_raw = [load_weight(w4, slice(0, H), slice(0, PASS), "w4_raw0", 0)]
        wl_raw = stream.tile([P, N], U32, name="wl_raw", offset=place)
        wl_raw_s = stream.tile([P, N], U8, name="wl_raw_s", offset=place + 4 * N)
        tab2_s = stream.tile([P, T2], U8, name="tab2_s", offset=place + 5 * N)
        load_words(wl_raw, wl_words[0])
        nc.gpsimd.memset(tab2_s[:].bitcast(I32), 0)
        nc.gpsimd.memset(wl_raw_s[:].bitcast(I32), 0)
        for q in range(4):
            nc.sync.dma_start(
                out=tab2_s[32 * q : 32 * q + 4, :].bitcast(I32), in_=tab2_scales[0, 4 * q : 4 * q + 4, :].bitcast(I32)
            )
        for q in range(4):
            nc.sync.dma_start(
                out=wl_raw_s[32 * q : 32 * q + 4, :].bitcast(I32), in_=wl_scales[0, 4 * q : 4 * q + 4, :].bitcast(I32)
            )
        tab2_w = stream.tile([P, T2], U32, name="tab2_w", offset=2 * place)
        load_words(tab2_w, tab2_words[0])
        w4_raw.append(load_weight(w4, slice(0, H), slice(PASS, N), "w4_raw1", 3))

        w2_codes, w2_planes = slices_of(w2_q)
        for u in range(halves):
            for t in range(PACK):
                acc = first_stage(w2_codes, w2_planes, t, u, "vector_banks")
                nc.vector.tensor_tensor(out=top[u][:, t, :], in0=acc[:], in1=top[u][:, t, :], op=ALU.max)

        def weave(dst, src, engine):
            copy_on(
                engine,
                dst.rearrange("p (c i t) -> p c t i", i=4, t=PACK),
                src.rearrange("p t (c i) -> p c t i", i=4),
            )

        w3_codes, w3_planes = slices_of(w3_q)
        h_rows = []
        for u in range(halves):
            rows = placed([P, PACK, BANK], BF16, "h_rows%d" % u, 8 + 2 * u)
            for t in range(PACK):
                acc = first_stage(w3_codes, w3_planes, t, u, ("scalar_banks", "vector_banks")[u])
                sine = placed([P, BANK], F32, "sine%d_%d" % (u, t), PACK * u + t)
                nc.scalar.activation(out=sine[:], in_=acc[:], func=ACT.Sin)
                nc.vector.scalar_tensor_tensor(
                    out=rows[:, t, :], in0=sine[:], scalar=gain_sb[:, t : t + 1], in1=top[u][:, t, :],
                    op0=ALU.mult, op1=ALU.add,
                )
            h_rows.append(rows)
        h_q = []
        for u, engines in enumerate((("scalar", "scalar"), ("scalar", "vector"))):
            grouped = placed([P, PACK * BANK], BF16, "h_rounded%d" % u, 14 + 2 * u)
            for i, engine in enumerate(engines):
                lo, hi = i * BANK // 2, (i + 1) * BANK // 2
                weave(grouped[:, PACK * lo : PACK * hi], h_rows[u][:, :, lo:hi], engine)
            h_q.append(quantise(grouped, "h%d" % u, 12 + u))

        w4_q = [quantise(round_weight(w4_raw[0], ("gpsimd",) * 4, rounded_tile(PACK * BANK, "early")), "w4_0")]

        v2_c = placed([P, PICKS], U32, "v2_c", 16)
        v2_s = placed([P, PICKS], U8, "v2_s", 17)
        nc.vector.tensor_copy(out=v2_s[:], in_=tab2_s[:].indirect(idx2[:]))
        nc.vector.tensor_copy(out=v2_c[:], in_=tab2_w[:].indirect(idx2[:]))
        wl_c = placed([P, N], U32, "wl_c", 2)
        wl_s = placed([P, N], U8, "wl_s", 17, PICKS)
        for g in range(groups):
            by_slice = wl_raw_s[:, g * PASS : (g + 1) * PASS].rearrange("p (m t) -> p t m", t=PACK)
            for t in range(PACK):
                nc.gpsimd.tensor_copy(out=wl_s[:, g * PASS + t * P : g * PASS + (t + 1) * P], in_=by_slice[:, t, :])
        deal(wl_c[:, 0:PASS], wl_raw[:, 0:PASS], "scalar")

        def scores(g, t):
            e_rows = ring.tile([P, S], F32, name="e_rows", tag="e_rows", bufs=8)
            codes, scales = w4_q[g]
            for u in range(halves):
                acc = psum.tile([P, BANK], F32, name="acc", tag="scalar_banks")
                nc.tensor.matmul_mx(
                    out=acc[:], lhsT=codes[:, t * P : (t + 1) * P].bitcast(FP8X4),
                    lhsT_scale=scales[:, t * P : (t + 1) * P],
                    rhs=h_q[u][0][:].bitcast(FP8X4), rhs_scale=h_q[u][1][:], start=True, stop=True,
                )
                nc.scalar.copy(out=e_rows[:, u * BANK : (u + 1) * BANK], in_=acc[:])
            return e_rows

        y = [held.tile([P, PACK, PICKS], F32, name="y", tag="wide", bufs=2) for g in range(groups)]
        y_c = keep([P, groups, PICKS], U32, "y_c")
        y_s = keep([P, groups, PICKS], U8, "y_s")

        def level_scores(g, t):
            acc = psum.tile([P, PICKS], F32, name="acc", tag="vector_banks")
            n_cols = slice(g * PASS + t * P, g * PASS + (t + 1) * P)
            nc.tensor.matmul_mx(
                out=acc[:], lhsT=wl_c[:, n_cols].bitcast(FP8X4), lhsT_scale=wl_s[:, n_cols],
                rhs=v2_c[:].bitcast(FP8X4), rhs_scale=v2_s[:], start=True, stop=True,
            )
            return acc

        def finish(g, t, lo, hi, adder):
            x, low = picked[(g, t)], lowered[(g, t)]
            adder.tensor_tensor(out=y[g][:, t, lo:hi], in0=low[:, lo:hi], in1=x[:, lo:hi], op=ALU.add)
            rows = out_0[g * PASS : (g + 1) * PASS, :].rearrange("(p t) j -> p t j", t=PACK)
            nc.sync.dma_start(out=rows[:, t, lo:hi], in_=y[g][:, t, lo:hi])

        def planes(g, lo, hi, engine):
            grouped = placed([P, PACK * PICKS], BF16, "y0_rounded", 12) if g == 0 else rounded_tile(PACK * (hi - lo), "late")
            weave(grouped[:], y[g][:, :, lo:hi], engine)
            nc.vector.quantize_mx(out=y_c[:, g, lo:hi].bitcast(FP8X4), scales=y_s[:, g, lo:hi], in_=grouped[:])
            nc.sync.dma_start(
                out=out_1[g, :, lo:hi, :].rearrange("p m i -> p (m i)").bitcast(I32), in_=y_c[:, g, lo:hi].bitcast(I32)
            )
            if hi == PICKS:
                for q in range(4):
                    (nc.sync, nc.scalar)[g * (q % 2)].dma_start(
                        out=out_2[g, 4 * q : 4 * q + 4, :].bitcast(I32),
                        in_=y_s[32 * q : 32 * q + 4, g, :].bitcast(I32),
                    )

        half = PICKS // 2
        e_tiles = {(0, t): scores(0, t) for t in range(2)}
        w4_q.append(quantise(round_weight(w4_raw[1], ("scalar", "scalar"), placed([P, PACK * BANK], BF16, "w4_1_rounded", 10)), "w4_1"))
        deal(wl_c[:, PASS:N], wl_raw[:, PASS:N], "scalar")
        for g, t in [(0, 2), (0, 3), (1, 0), (1, 1), (1, 2), (1, 3)]:
            e_tiles[(g, t)] = scores(g, t)

        picked, lowered, levels = {}, {}, {}

        def pair(pieces):
            for g, t, lo in pieces:
                if (g, t) not in picked:
                    picked[(g, t)] = ring.tile([P, PICKS], F32, name="picked", tag="picked", bufs=4)
                    lowered[(g, t)] = ring.tile([P, PICKS], F32, name="lowered", tag="lowered", bufs=4)
                    levels[(g, t)] = level_scores(g, t)
                nc.vector.tensor_copy(
                    out=picked[(g, t)][:, lo : lo + half],
                    in_=e_tiles[(g, t)][:].indirect(pick[:, lo // 16 : (lo + half) // 16]),
                )
            for g, t, lo in pieces:
                cols = slice(lo, lo + half)
                nc.vector.tensor_tensor(
                    out=lowered[(g, t)][:, cols], in0=levels[(g, t)][:, cols], in1=picked[(g, t)][:, cols], op=ALU.min
                )

        for g, t in [(0, 0), (0, 1), (0, 2), (0, 3), (1, 0), (1, 1)]:
            pair([(g, t, 0), (g, t, half)])
            finish(g, t, 0, PICKS, nc.gpsimd)
            if (g, t) == (0, PACK - 1):
                planes(0, 0, PICKS, "scalar")
        for lo, adder, weaver in ((0, nc.gpsimd, "scalar"), (half, nc.vector, "vector")):
            pair([(1, 2, lo), (1, 3, lo)])
            for t in (2, 3):
                finish(1, t, lo, lo + half, adder)
            planes(1, lo, lo + half, weaver)
